import numpy as np, ml_dtypes
CORES = [48,51,52,55]
N = 4
BF = ml_dtypes.bfloat16
def gentries(a):
    return np.ascontiguousarray(a.reshape(8, 16, -1).transpose(0, 2, 1)).reshape(8, -1)
def gtable(e):
    e = np.asarray(e); return np.ascontiguousarray(e.reshape(8, -1, 16).transpose(0, 2, 1)).reshape(128, -1).astype(np.int32)
D, UG, B, A, NB, KG = 2, 16, 6, 2, 64, 32
U, V, E, S, K = 8 * UG, 2 ** B, 2 ** (A * B), 16 * NB, 8 * KG // N
def stored(c):
    return np.ascontiguousarray(c.reshape(N, 8, UG, NB, 16).transpose(0, 1, 4, 3, 2)).reshape(N, 128, -1).astype(np.int32)
def unstored(x):
    return np.ascontiguousarray(x.reshape(N, 8, 16, NB, UG).transpose(0, 1, 4, 3, 2)).reshape(N, U, S).astype(np.int64)
def pack(t, c, gv, wr):
    return {"tb": t.reshape(N, 8, -1).astype(np.float32).astype(BF), "x": stored(c), "give": np.stack([gtable(v.reshape(8, -1)) for v in gv]), "wires": np.stack([gtable(v.reshape(8, -1)) for v in wr])}
def draw(rng):
    return rng.integers(0, V, (N, 8, D, UG, E)), rng.integers(0, V, (N, U, S)), rng.integers(0, U, (N, 8, D, KG)), rng.integers(0, N * K, (N, 8, D, A, UG))
def setup_inputs(rng):
    return pack(*draw(rng))
def setup_inputs_ends(rng):
    t, c, gv, wr = draw(rng)
    t = rng.integers(0, 2, t.shape) * (V - 1); t[..., 0] = 0; t[..., E - 1] = V - 1; c = rng.integers(0, 2, c.shape) * (V - 1); c[:, :, 0] = 0; c[:, :, S - 1] = V - 1
    gv = rng.choice(np.array([0, UG - 1, UG, 7 * UG, U - 1]), gv.shape); wr = rng.choice(np.array([0, K - 1, K, N * K - K, N * K - 1]), wr.shape)
    return pack(t, c, gv, wr)
def setup_inputs_one(rng):
    t, c, gv, wr = draw(rng)
    gv[:] = gv[..., :1].copy(); wr[:] = wr[:, :, :, :1].copy(); q = rng.integers(0, N); wr[q] = wr[q][..., :1].copy()
    return pack(t, c, gv, wr)
def setup_inputs_next(rng):
    t, c, gv, wr = draw(rng)
    i = rng.integers(0, 2, (N, 8, D, UG, 1)) * (A - 1); t = (np.arange(E) >> (B * (A - 1 - i))) & (V - 1)
    wr = wr % K + K * ((np.arange(N) + 1) % N).reshape(N, 1, 1, 1, 1)
    return pack(t, c, gv, wr)
def setup_inputs_spread(rng):
    t, c, gv, wr = draw(rng)
    t = t >> rng.integers(0, B + 1, (N, 8, D, UG, 1)); c = c >> rng.integers(0, B + 1, (N, U, 1))
    gv = (rng.random(gv.shape) ** 3 * U).astype(np.int64); wr = (rng.random(wr.shape) ** 3 * (N * K)).astype(np.int64)
    return pack(t, c, gv, wr)
def check_inputs(d):
    bad = []
    for name, top in (("x", V), ("give", U), ("wires", N * K)):
        if not ((d[name] >= 0) & (d[name] < top)).all(): bad.append(name)
    t = d["tb"].astype(np.float32)
    if not ((t >= 0) & (t < V) & (np.floor(t) == t)).all(): bad.append("tb")
    return bad
def reference(tb, x, give, wires):
    t = tb.astype(np.float32).astype(np.int64).reshape(N, 8, D, UG, E)
    gv = np.stack([gentries(v) for v in give]).reshape(N, 8 * D * KG).reshape(N, 8, D, KG)
    wr = np.stack([gentries(v) for v in wires]).reshape(N, 8, D, A, UG)
    c = unstored(x)
    for l in range(D):
        lines = np.zeros((N, N * K, S), np.int64); new = np.zeros((N, U, S), np.int64)
        for q in range(N):
            lines[:, q * K:(q + 1) * K] = c[q][gv[q, :, l].reshape(-1)].reshape(N, K, S)
        for r in range(N):
            a = np.zeros((8, UG, S), np.int64)
            for i in range(A):
                a = a * V + lines[r][wr[r, :, l, i]]
            new[r] = np.take_along_axis(t[r, :, l], a, axis=2).reshape(U, S)
        c = new
    return {"y": np.asarray(stored(c), np.float32)}

@@ -1,0 +1,403 @@
+from concourse.bass import DstId, RemoteDMATransfer
+from concourse.mybir import AluOpType as OP, ActivationFunctionType as ACT
+
+NCH = 4
+CS = 256
+SPL = [[124, 132, 126, 126], [122, 122, 128, 0]]
+SA = 11
+
+SCRATCH = {
+    "xi": ("sbuf", [128, 1024], "int32"),
+    "xb": ("sbuf", [128, 1024], "bfloat16"),
+    "yt": ("sbuf", [128, 1024], "bfloat16"),
+    "gs": ("sbuf", [128, 4], "int32"),
+    "gl": ("sbuf", [128, 16], "int32"),
+    "giv": ("sbuf", [128, 4], "float32"),
+    "wi": ("sbuf", [128, 4], "int32"),
+    "wf": ("sbuf", [128, 4], "float32"),
+    "pcol": ("sbuf", [128, 1], "int32"),
+    "kbi": ("sbuf", [128, 1], "int32"),
+    "kbf": ("sbuf", [128, 2], "float32"),
+    "ones": ("sbuf", [128, 512], "bfloat16"),
+    "diff": ("sbuf", [128, 128], "bfloat16"),
+    "iotn": ("sbuf", [128, 128], "bfloat16"),
+    "iotl": ("sbuf", [128, 256], "bfloat16"),
+    "ident": ("sbuf", [128, 128], "bfloat16"),
+    "pm": ("sbuf", [128, 512], "bfloat16"),
+    "lm": ("sbuf", [128, 2048], "bfloat16"),
+    "rm": ("sbuf", [128, 128], "bfloat16"),
+    "vt": ("sbuf", [128, 1024], "bfloat16"),
+    "vb": ("sbuf", [128, 512], "bfloat16"),
+    "gt": ("sbuf", [128, 512], "bfloat16"),
+    "w": ("sbuf", [128, 1024], "bfloat16"),
+    "c0": ("sbuf", [128, 4096], "bfloat16"),
+    "c1": ("sbuf", [128, 4096], "bfloat16"),
+    "tab0": ("sbuf", [128, 4096], "bfloat16"),
+    "tab1": ("sbuf", [128, 4096], "bfloat16"),
+    "off0": ("sbuf", [128, 1024], "uint16"),
+    "off1": ("sbuf", [128, 1024], "uint16"),
+    "ga0": ("sbuf", [128, 16384], "bfloat16"),
+    "ga1": ("sbuf", [128, 16384], "bfloat16"),
+    "ys": ("sbuf", [128, 1024], "float32"),
+    "yl": ("sbuf", [128, 256], "float32"),
+    "psv": ("psum", [128, 512], "float32"),
+    "psw": ("psum", [128, 512], "float32"),
+    "psf0": ("psum", [128, 512], "float32"),
+    "psf1": ("psum", [128, 512], "float32"),
+    "psa0": ("psum", [128, 512], "float32"),
+    "psa1": ("psum", [128, 512], "float32"),
+    "psc0": ("psum", [128, 512], "float32"),
+    "psc1": ("psum", [128, 512], "float32"),
+}
+SEMAPHORES = (["dx0", "dxr", "dgv", "dwr", "dt0", "dt1", "dy", "iop", "iod", "iol", "ion", "von", "lmg", "rmg",
+               "vi", "vf", "vid", "vpm", "vwf", "vvt0", "vvt1", "vgiv", "vgt0", "vgt1", "pv0", "pv1", "sv0", "sv1",
+               "pwv", "pws", "pw1", "swv", "sws", "sw1", "agv", "loc", "cv0", "cv1", "cv2", "tr0", "tr1", "tr2"]
+              + ["%s%d" % (a, c) for c in range(NCH) for a in ("pf", "ce", "ac", "bc", "sc")]
+              + ["%s%d%d" % (a, l, c) for l in range(2) for c in range(NCH) for a in ("pa", "ea")]
+              + ["%s%d%d" % (a, l, c) for l in range(2) for c in range(NCH + l) for a in ("gv", "gs", "pd")]
+              + ["sy%d" % c for c in range(NCH + 1)])
+
+
+def rank_program(g, core, T, topo):
+    rank = T.rank_of(core)
+    if rank is None:
+        return
+    V, S, P, Y = g.vector, g.scalar, g.tensor, g.sync
+    sem = T.sem
+    others = [c for c in T.cores if c != core]
+    n_oth = len(others)
+    engs = topo.engines(core, others[0])
+    for c in others:
+        engs = [e for e in engs if e in topo.engines(core, c)]
+    ne = len(engs)
+    emask = sum(1 << e for e in engs)
+    ids = []
+    for c in others:
+        a = topo.addr(c)
+        ids.append(DstId(rid=a[0], pnc=a[1]))
+
+    def bcast(src, dst, name):
+        g.remote_dma_fused([RemoteDMATransfer(dst_ids=ids, dma_engine_mask=emask, remote_sem=sem[name],
+                                              srcs=[src], dsts=[dst] * n_oth)], local_sem=sem.loc)
+
+    own = rank * 1024
+    psf, psa, psc = [T.psf0, T.psf1], [T.psa0, T.psa1], [T.psc0, T.psc1]
+    cb, tab, off, ga = [T.c0, T.c1], [T.tab0, T.tab1], [T.off0, T.off1], [T.ga0, T.ga1]
+    psw = [[T.psc0, T.psc1, T.psw, T.psa1], [T.psw] * 4]
+    psv = [T.psv, T.psa0]
+
+    S.dma_start(T.gs[:], T.give[:]).then_inc(sem.dgv, 16)
+    Y.dma_start(T.xi[:, 0:CS], T.x[:, 0:CS]).then_inc(sem.dx0, 16)
+    S.dma_start(T.wi[:], T.wires[:]).then_inc(sem.dwr, 16)
+    Y.dma_start(T.xi[:, CS:1024], T.x[:, CS:1024]).then_inc(sem.dxr, 16)
+    Y.dma_start(T.tab0[0:64, :], T.tb[0:4, 0:65536]).then_inc(sem.dt0, 16)
+    Y.wait_ge(sem.dxr, 16)
+    Y.dma_start(T.tab0[64:128, :], T.tb[4:8, 0:65536]).then_inc(sem.dt0, 16)
+
+    lax = {"allow_small_or_imprecise_dtypes": True}
+    g.iota(T.pcol[:], [[1, 1]], 0, 1).then_inc(sem.iop, 1)
+    g.iota(T.diff[:], [[1, 128]], 0, -1, **lax).then_inc(sem.iod, 1)
+    g.iota(T.iotl[:], [[16, 2], [32, 8], [1, 16]], 0, 0, **lax).then_inc(sem.iol, 1)
+    g.iota(T.iotn[:], [[1, 128]], 0, 0, **lax).then_inc(sem.ion, 1)
+
+    def masks(i):
+        g.affine_select(T.lm[:, 512 * i:512 * i + 512], T.ones[:], [[1000, 4], [-16, 8], [-1001, 16]], OP.is_equal, 0.0,
+                        4000 * i, 1).then_inc(sem.lmg, 1)
+
+    def send(l, c):
+        g.wait_ge(sem["%s%d" % ("sc" if l else "ce", c)], 1)
+        a = own + c * CS
+        bcast(cb[l][:, a:a + CS], cb[l][:, a:a + CS], "%s%d" % ("bc" if l else "ac", c))
+
+    g.wait_ge(sem.dgv, 16)
+    bcast(T.gs[:], T.gl[:, 4 * rank:4 * rank + 4], "agv")
+    send(0, 0)
+    g.wait_ge(sem.von, 1)
+    masks(0)
+    send(0, 1)
+    masks(1)
+    send(0, 2)
+    masks(2)
+    masks(3)
+    send(0, 3)
+    g.affine_select(T.rm[:], T.ones[:, 0:128], [[-1, 16], [-16, 8]], OP.is_equal, 0.0, 0, 1).then_inc(sem.rmg, 1)
+    for c in range(NCH):
+        send(1, c)
+    g.wait_ge(sem.loc, ne * (1 + 2 * NCH))
+
+    def onehot_wires(l, i):
+        k = 2 * l + i
+        V.tensor_scalar(T.vt[:, 256 * k:256 * k + 256], T.iotl[:], T.wf[:, k:k + 1], 64.0 if i == 0 else 1.0,
+                        OP.is_equal, OP.mult).then_inc(sem["vvt%d" % l], 1)
+
+    def onehot_give(l):
+        for k in (2 * l, 2 * l + 1):
+            V.tensor_scalar(T.gt[:, 128 * k:128 * k + 128], T.iotn[:], T.giv[:, k:k + 1], None, OP.is_equal).then_inc(sem["vgt%d" % l], 1)
+
+    def fix(c, halves=(0, 1)):
+        P.wait_ge(sem["tr%d" % min(c, 2)], 1 if c else 8)
+        if c == 0:
+            P.wait_ge(sem.vpm, 4)
+        if c >= 2:
+            P.wait_ge(sem["ce%d" % (c - 2)], 1)
+        for h in halves:
+            for bp in range(8 if c else 1):
+                for g2 in range(2):
+                    k = 2 * g2 + h
+                    if c:
+                        i0 = c * CS + 32 * bp + 16 * g2
+                        o, i = psf[c % 2][:, 128 * h + bp:128 * h + 128:8], T.yt[:, i0:i0 + 16]
+                    else:
+                        o, i = psf[0][:, 128 * h:128 * h + 128], T.yt[:, 128 * g2:128 * g2 + 128]
+                    m = P.matmul(o, T.pm[:, 128 * k:128 * k + 128], i, g2 == 0, g2 == 1)
+            m.then_inc(sem["pf%d" % c], 1)
+
+    def compose_v(l):
+        P.wait_ge(sem["vvt%d" % l], 2)
+        for kh in range(2):
+            for i in range(2):
+                a = (2 * l + i) * 256 + 128 * kh
+                m = P.matmul(psv[l][:, 128 * kh:128 * kh + 128], T.vt[:, a:a + 128], T.ident[:], i == 0, i == 1)
+                if i == 1:
+                    m.then_inc(sem["pv%d" % l], 1)
+
+    def w_part(l, q, kh):
+        a = 128 * q if l else 0
+        return P.matmul(psw[l][q][:, a:a + 128],
+                        T.gt[32 * q:32 * q + 32, (2 * l + kh) * 128:(2 * l + kh) * 128 + 128],
+                        T.vb[32 * q:32 * q + 32, l * 256 + 128 * kh:l * 256 + 128 * kh + 128], kh == 0, kh == 1)
+
+    def compose_w0():
+        P.wait_ge(sem.sv0, 1)
+        for kh in range(2):
+            P.wait_ge(sem.vgt0, kh + 1)
+            for q in range(4):
+                m = w_part(0, q, kh)
+                if kh:
+                    m.then_inc(sem["pwv" if q < 3 else "pws"], 1)
+
+    def compose_w1():
+        P.wait_ge(sem.vgt1, 2)
+        P.wait_ge(sem.sv1, 1)
+        for q in range(4):
+            if q:
+                P.wait_ge(sem.pw1, q)
+            w_part(1, q, 0)
+            w_part(1, q, 1).then_inc(sem.pw1, 1)
+
+    def addresses(l, c):
+        P.wait_ge(sem["%s%d" % ("ce" if l == 0 else "sc", c)], 1)
+        P.wait_ge(sem["%s%d" % ("ac" if l == 0 else "bc", c)], ne * n_oth)
+        if c == 0:
+            P.wait_ge(sem.sw1 if l else sem.sv1, 1)
+        k = l * NCH + c - 2
+        if k >= 0:
+            P.wait_ge(sem["ea%d%d" % (k // NCH, k % NCH)], 2)
+        for q in range(4):
+            if l == 0 and c == 0:
+                P.wait_ge(sem.swv if q < 3 else sem.sws, q + 1 if q < 3 else 1)
+            m = P.matmul(psa[c % 2][:, 0:CS], T.w[:, (4 * l + q) * 128:(4 * l + q) * 128 + 128],
+                         cb[l][:, q * 1024 + c * CS:q * 1024 + (c + 1) * CS], q == 0, q == 3)
+        m.then_inc(sem["pa%d%d" % (l, c)], 1)
+
+    def gpos(l, c, h):
+        if l == 0 or c < NCH - 1:
+            nv = SPL[l][c]
+            return (c * CS + nv, (c + 1) * CS) if h else (c * CS, c * CS + nv)
+        o = (NCH - 1) * CS + 128 * h
+        return (o, o + 8 * SA) if c == NCH - 1 else (o + 8 * SA, o + 128)
+
+    def tile(c, h):
+        return gpos(1, c, h) if c >= NCH - 1 else (c * CS + 128 * h, c * CS + 128 * h + 128)
+
+    def pick(l, c):
+        if c == 0:
+            if l:
+                P.wait_ge(sem.rmg, 1)
+            else:
+                P.wait_ge(sem.lmg, 4)
+        k = l * NCH + c - 2
+        if k >= 0:
+            P.wait_ge(sem["%s%d" % ("sc" if k < NCH else "sy", k % NCH)], 1)
+        for h in range(2):
+            P.wait_ge(sem["%s%d%d" % ("gs" if h else "gv", l, c)], 1)
+            j0, j1 = tile(c, h) if l else gpos(0, c, h)
+            if l and h == 0 and j1 > gpos(1, c, 0)[1]:
+                P.wait_ge(sem["gs%d%d" % (l, c)], 1)
+            for u in range(16):
+                src = ga[l][:, 16 * j0 + u:16 * j1:16]
+                if l == 0:
+                    m = P.matmul(psc[c % 2][:, j0 - c * CS:j1 - c * CS], T.lm[:, 128 * u:128 * u + 128], src, u == 0, u == 15)
+                else:
+                    m = P.matmul(psc[c % 2][0:j1 - j0, 16 * h + u:256:32], src, T.rm[:, 8 * u:8 * u + 8], True, True)
+            m.then_inc(sem["pd%d%d" % (l, c)], 1)
+
+    def evac_addr(l, c):
+        V.wait_ge(sem["pa%d%d" % (l, c)], 1)
+        for a, b in (gpos(l, c, 0), gpos(l, c, 1)) if SPL[l][c] else ((c * CS, (c + 1) * CS),):
+            V.tensor_copy(off[l][:, a:b], psa[c % 2][:, a - c * CS:b - c * CS]).then_inc(sem["ea%d%d" % (l, c)], 1)
+
+    def gather(l, c, h):
+        q = S if h else V
+        q.wait_ge(sem["ea%d%d" % (l, min(c, NCH - 1))], 2 if h and SPL[l][min(c, NCH - 1)] else 1)
+        if c == 0:
+            q.wait_ge(sem["dt%d" % l], 16 if l else 32)
+        j0, j1 = gpos(l, c, h)
+        win = tab[l][:, 0:4096].indirect(off[l][:, j0:j1])
+        if h == 0:
+            V.tensor_copy(ga[l][:, 16 * j0:16 * j1], win).then_inc(sem["gv%d%d" % (l, c)], 1)
+        else:
+            S.activation(ga[l][:, 16 * j0:16 * j1], win, ACT.Copy).then_inc(sem["gs%d%d" % (l, c)], 1)
+
+    def s_c0(c):
+        S.wait_ge(sem["pf%d" % c], 2)
+        S.activation(T.c0[:, own + c * CS:own + (c + 1) * CS], psf[c % 2][:, 0:CS], ACT.Copy).then_inc(sem["ce%d" % c], 1)
+
+    def s_c1(c):
+        S.wait_ge(sem["pd0%d" % c], 2)
+        S.activation(T.c1[:, own + c * CS:own + (c + 1) * CS], psc[c % 2][:, 0:CS], ACT.Copy).then_inc(sem["sc%d" % c], 1)
+
+    def ysrc(c):
+        if c < NCH - 1:
+            return T.ys, c * CS, 128
+        return (T.ys, (NCH - 1) * CS, 8 * SA) if c == NCH - 1 else (T.yl, 0, 128 - 8 * SA)
+
+    def out_y(q, c):
+        q.wait_ge(sem["pd1%d" % c], 2)
+        b, a, n = ysrc(c)
+        if q is V:
+            m = V.tensor_copy(b[0:n, a:a + CS], psc[c % 2][0:n, 0:CS])
+        else:
+            m = S.activation(b[0:n, a:a + CS], psc[c % 2][0:n, 0:CS], ACT.Copy)
+        m.then_inc(sem["sy%d" % c], 1)
+
+    V.memset(T.ones[:], 1.0).then_inc(sem.von, 1)
+    V.wait_ge(sem.iop, 1)
+    V.tensor_scalar(T.kbi[:], T.pcol[:], 4, 1, OP.logical_shift_right, OP.bitwise_and).then_inc(sem.vi, 1)
+    V.wait_ge(sem.vi, 1)
+    V.tensor_copy(T.kbf[:, 1:2], T.kbi[:]).then_inc(sem.vf, 1)
+    V.tensor_scalar(T.kbf[:, 0:1], T.kbi[:], -1.0, 1.0, OP.mult, OP.add).then_inc(sem.vf, 1)
+    V.wait_ge(sem.iod, 1)
+    V.tensor_scalar(T.ident[:], T.diff[:], 0.0, None, OP.is_equal).then_inc(sem.vid, 1)
+    V.wait_ge(sem.vf, 2)
+    for g2 in range(2):
+        for h in range(2):
+            k = 2 * g2 + h
+            V.tensor_scalar(T.pm[:, 128 * k:128 * k + 128], T.diff[:], float(16 * (g2 - h)), T.kbf[:, h:h + 1],
+                            OP.is_equal, OP.mult).then_inc(sem.vpm, 1)
+    V.wait_ge(sem.dx0, 16)
+    for h in range(2):
+        V.tensor_copy(T.xb[:, 128 * h:128 * h + 128], T.xi[:, 128 * h:128 * h + 128]).then_inc(sem.cv0, 1)
+    V.wait_ge(sem.dwr, 16)
+    V.tensor_copy(T.wf[:], T.wi[:]).then_inc(sem.vwf, 1)
+    for bp in range(8):
+        V.wait_ge(sem.cv0, 1 + bp // 4)
+        V.transpose(T.yt[:, bp:CS:8], T.xb[:, 32 * bp:32 * bp + 32]).then_inc(sem.tr0, 1)
+    V.wait_ge(sem.iol, 1)
+    V.wait_ge(sem.vwf, 1)
+    onehot_wires(0, 0)
+    V.wait_ge(sem.dxr, 16)
+    V.tensor_copy(T.xb[:, CS:2 * CS], T.xi[:, CS:2 * CS]).then_inc(sem.cv1, 1)
+    onehot_wires(0, 1)
+    V.wait_ge(sem.cv1, 1)
+    V.transpose(T.yt[:, CS:2 * CS], T.xb[:, CS:2 * CS]).then_inc(sem.tr1, 1)
+    V.tensor_copy(T.xb[:, 2 * CS:1024], T.xi[:, 2 * CS:1024]).then_inc(sem.cv2, 1)
+    onehot_wires(1, 0)
+    onehot_wires(1, 1)
+    V.wait_ge(sem.cv2, 1)
+    V.transpose(T.yt[:, 2 * CS:1024], T.xb[:, 2 * CS:1024]).then_inc(sem.tr2, 1)
+    V.wait_ge(sem.ion, 1)
+    V.wait_ge(sem.dgv, 16)
+    V.wait_ge(sem.agv, ne * n_oth)
+    for q in range(4):
+        r0 = 32 * rank
+        src = T.gs[r0:r0 + 32, 0:4] if q == rank else T.gl[r0:r0 + 32, 4 * q:4 * q + 4]
+        V.tensor_copy(T.giv[32 * q:32 * q + 32, 0:4], src).then_inc(sem.vgiv, 1)
+    V.wait_ge(sem.vgiv, 4)
+    onehot_give(0)
+    for q in range(3):
+        V.wait_ge(sem.pwv, q + 1)
+        V.tensor_copy(T.w[:, 128 * q:128 * q + 128], psw[0][q][:, 0:128]).then_inc(sem.swv, 1)
+    onehot_give(1)
+    for c in range(NCH):
+        evac_addr(0, c)
+        gather(0, c, 0)
+    for c in range(NCH):
+        evac_addr(1, c)
+        if c == NCH - 1:
+            out_y(V, 1)
+        gather(1, c, 0)
+    out_y(V, 2)
+    gather(1, 4, 0)
+    out_y(V, 3)
+    out_y(V, 4)
+
+    s_c0(0)
+    S.wait_ge(sem.pv0, 2)
+    S.activation(T.vb[:, 0:256], psv[0][:, 0:256], ACT.Copy).then_inc(sem.sv0, 1)
+    s_c0(1)
+    S.wait_ge(sem.pv1, 2)
+    S.activation(T.vb[:, 256:512], psv[1][:, 0:256], ACT.Copy).then_inc(sem.sv1, 1)
+    S.wait_ge(sem.pws, 1)
+    S.activation(T.w[:, 384:512], psw[0][3][:, 0:128], ACT.Copy).then_inc(sem.sws, 1)
+    s_c0(2)
+    gather(0, 0, 1)
+    s_c0(3)
+    S.wait_ge(sem.pw1, 4)
+    S.activation(T.w[:, 512:1024], T.psw[:], ACT.Copy).then_inc(sem.sw1, 1)
+    gather(0, 1, 1)
+    s_c1(0)
+    gather(0, 2, 1)
+    s_c1(1)
+    gather(0, 3, 1)
+    s_c1(2)
+    gather(1, 0, 1)
+    s_c1(3)
+    gather(1, 1, 1)
+    out_y(S, 0)
+    gather(1, 2, 1)
+    gather(1, 3, 1)
+    gather(1, 4, 1)
+
+    P.wait_ge(sem.vid, 1)
+    fix(0)
+    compose_v(0)
+    fix(1)
+    compose_v(1)
+    fix(2, (0,))
+    compose_w0()
+    fix(2, (1,))
+    addresses(0, 0)
+    fix(3)
+    compose_w1()
+    addresses(0, 1)
+    pick(0, 0)
+    addresses(0, 2)
+    pick(0, 1)
+    addresses(0, 3)
+    pick(0, 2)
+    addresses(1, 0)
+    pick(0, 3)
+    addresses(1, 1)
+    pick(1, 0)
+    addresses(1, 2)
+    pick(1, 1)
+    addresses(1, 3)
+    pick(1, 2)
+    pick(1, 3)
+    pick(1, 4)
+
+    Y.wait_ge(sem.ea00, 2)
+    Y.dma_start(T.tab1[:], T.tb[:, 65536:131072]).then_inc(sem.dt1, 16)
+    for c in range(NCH + 1):
+        last = c >= NCH - 1
+        Y.wait_ge(sem["sy%d" % c], 1)
+        if last:
+            S.wait_ge(sem["sy%d" % c], 1)
+        b, a, n = ysrc(c)
+        cc = min(c, NCH - 1)
+        for gg in range(8):
+            q = S if last and gg % 2 else Y
+            r0 = 16 * gg + (SA if c == NCH else 0)
+            q.dma_start(T.y[r0:r0 + n // 8, cc * CS:(cc + 1) * CS], b[0:n, a + 32 * gg:a + 32 * gg + 32]).then_inc(sem.dy, 16)
+    Y.wait_ge(sem.dy, 16 * 8 * (NCH + 1))

@@ -3,32 +3,37 @@ from concourse.mybir import AluOpType as OP, ActivationFunctionType as ACT
 
 NCH = 4
 CS = 256
-SPL = [[124, 132, 126, 126], [122, 122, 128, 0]]
-SA = 11
+SPL = [[122, 118, 136, 128], [128, 128, 128]]
+TAIL = [[(0, 86), (160, 210)], [(86, 160), (210, 256)]]
+OUT = [(0, 10, 0, "YS"), (10, 16, 2, "YS")]
+GDIV = 2
+YO = "l0 l1 l2 T003 i1 T038 p1 T108"
+GO = "i x24 s12 m s24"
+VE = "x12 t12"
+VO = "o1 t24 v1 v3 a00 g00 b01 b02 g01 g02 a03 g03 a10 g10 a11 g11 a12 g12 a13 g13 g14 y4"
+SO = "w03 g00 g01 c0 g02 c1 g03 c2 g10 c3 g11 y0 g12 y1 g13 y2 g14 y3 z3 z4"
+PO = "w04 a00 a01 a02 p00 a03 p01 p020 a10 p021 p030 a11 p031 p10 a12 p11 a13 p12 p13 p14"
+BANKS = "57567567"
 
 SCRATCH = {
     "xi": ("sbuf", [128, 1024], "int32"),
     "xb": ("sbuf", [128, 1024], "bfloat16"),
-    "yt": ("sbuf", [128, 1024], "bfloat16"),
     "gs": ("sbuf", [128, 4], "int32"),
     "gl": ("sbuf", [128, 16], "int32"),
     "giv": ("sbuf", [128, 4], "float32"),
     "wi": ("sbuf", [128, 4], "int32"),
-    "wf": ("sbuf", [128, 4], "float32"),
-    "pcol": ("sbuf", [128, 1], "int32"),
-    "kbi": ("sbuf", [128, 1], "int32"),
-    "kbf": ("sbuf", [128, 2], "float32"),
+    "wf": ("sbuf", [128, 8], "float32"),
     "ones": ("sbuf", [128, 512], "bfloat16"),
+    "step": ("sbuf", [128, 256], "bfloat16"),
     "diff": ("sbuf", [128, 128], "bfloat16"),
-    "iotn": ("sbuf", [128, 128], "bfloat16"),
+    "iotn": ("sbuf", [128, 256], "bfloat16"),
     "iotl": ("sbuf", [128, 256], "bfloat16"),
     "ident": ("sbuf", [128, 128], "bfloat16"),
-    "pm": ("sbuf", [128, 512], "bfloat16"),
-    "lm": ("sbuf", [128, 2048], "bfloat16"),
-    "rm": ("sbuf", [128, 128], "bfloat16"),
+    "zm": ("sbuf", [128, 512], "bfloat16"),
     "vt": ("sbuf", [128, 1024], "bfloat16"),
     "vb": ("sbuf", [128, 512], "bfloat16"),
     "gt": ("sbuf", [128, 512], "bfloat16"),
+    "gto": ("sbuf", [128, 256], "bfloat16"),
     "w": ("sbuf", [128, 1024], "bfloat16"),
     "c0": ("sbuf", [128, 4096], "bfloat16"),
     "c1": ("sbuf", [128, 4096], "bfloat16"),
@@ -38,24 +43,16 @@ SCRATCH = {
     "off1": ("sbuf", [128, 1024], "uint16"),
     "ga0": ("sbuf", [128, 16384], "bfloat16"),
     "ga1": ("sbuf", [128, 16384], "bfloat16"),
-    "ys": ("sbuf", [128, 1024], "float32"),
-    "yl": ("sbuf", [128, 256], "float32"),
-    "psv": ("psum", [128, 512], "float32"),
-    "psw": ("psum", [128, 512], "float32"),
-    "psf0": ("psum", [128, 512], "float32"),
-    "psf1": ("psum", [128, 512], "float32"),
-    "psa0": ("psum", [128, 512], "float32"),
-    "psa1": ("psum", [128, 512], "float32"),
-    "psc0": ("psum", [128, 512], "float32"),
-    "psc1": ("psum", [128, 512], "float32"),
+    "ys": ("sbuf", [128, 1792], "float32"),
 }
-SEMAPHORES = (["dx0", "dxr", "dgv", "dwr", "dt0", "dt1", "dy", "iop", "iod", "iol", "ion", "von", "lmg", "rmg",
-               "vi", "vf", "vid", "vpm", "vwf", "vvt0", "vvt1", "vgiv", "vgt0", "vgt1", "pv0", "pv1", "sv0", "sv1",
-               "pwv", "pws", "pw1", "swv", "sws", "sw1", "agv", "loc", "cv0", "cv1", "cv2", "tr0", "tr1", "tr2"]
-              + ["%s%d" % (a, c) for c in range(NCH) for a in ("pf", "ce", "ac", "bc", "sc")]
+SCRATCH.update({"b%d" % i: ("psum", [128, 512], "float32") for i in range(8)})
+SEMAPHORES = (["dgv", "dwr", "dxs", "dy", "iod", "iol", "ion", "von", "vst", "vwn", "sab", "zmg", "vid", "vwf",
+               "vvt0", "vvt1", "vgio", "vgto", "vgiv", "vgt0", "vgt1", "pv0", "pv1", "sv0", "sv1", "pw1", "sw1", "agv",
+               "loc", "gone"]
+              + ["%s%d" % (a, c) for c in range(NCH) for a in ("dx", "cv", "tr", "ac", "pw0", "sw0", "bc", "sc")]
               + ["%s%d%d" % (a, l, c) for l in range(2) for c in range(NCH) for a in ("pa", "ea")]
-              + ["%s%d%d" % (a, l, c) for l in range(2) for c in range(NCH + l) for a in ("gv", "gs", "pd")]
-              + ["sy%d" % c for c in range(NCH + 1)])
+              + ["%s%d%d" % (a, l, c) for l in range(2) for c in range(NCH + 4 * l) for a in ("gv", "gs", "pd")]
+              + ["sy%d" % c for c in range(NCH + 3)] + ["dt" + w[1:3] for w in YO.split() if w[0] == "T"])
 
 
 def rank_program(g, core, T, topo):
@@ -70,87 +67,62 @@ def rank_program(g, core, T, topo):
     for c in others:
         engs = [e for e in engs if e in topo.engines(core, c)]
     ne = len(engs)
-    emask = sum(1 << e for e in engs)
-    ids = []
-    for c in others:
-        a = topo.addr(c)
-        ids.append(DstId(rid=a[0], pnc=a[1]))
+    ng = ne // GDIV
+    ids = [DstId(rid=topo.addr(c)[0], pnc=topo.addr(c)[1]) for c in others]
+    sent = [0]
 
-    def bcast(src, dst, name):
-        g.remote_dma_fused([RemoteDMATransfer(dst_ids=ids, dma_engine_mask=emask, remote_sem=sem[name],
+    def write(src, dst, name, engines):
+        g.remote_dma_fused([RemoteDMATransfer(dst_ids=ids, dma_engine_mask=sum(1 << e for e in engines), remote_sem=sem[name],
                                               srcs=[src], dsts=[dst] * n_oth)], local_sem=sem.loc)
+        sent[0] += len(engines)
 
     own = rank * 1024
-    psf, psa, psc = [T.psf0, T.psf1], [T.psa0, T.psa1], [T.psc0, T.psc1]
+    B = [T["b%d" % i] for i in range(8)]
     cb, tab, off, ga = [T.c0, T.c1], [T.tab0, T.tab1], [T.off0, T.off1], [T.ga0, T.ga1]
-    psw = [[T.psc0, T.psc1, T.psw, T.psa1], [T.psw] * 4]
-    psv = [T.psv, T.psa0]
+    qs = [rank] + [q for q in range(4) if q != rank]
+    psv, psw1 = [B[4], B[7]], B[4]
+    last, half = NCH - 1, CS // 2
+    psc = [B[0], B[1], B[0], B[1], B[2], B[3], B[2], B[0], B[1], B[4], B[3]]
 
-    S.dma_start(T.gs[:], T.give[:]).then_inc(sem.dgv, 16)
-    Y.dma_start(T.xi[:, 0:CS], T.x[:, 0:CS]).then_inc(sem.dx0, 16)
-    S.dma_start(T.wi[:], T.wires[:]).then_inc(sem.dwr, 16)
-    Y.dma_start(T.xi[:, CS:1024], T.x[:, CS:1024]).then_inc(sem.dxr, 16)
-    Y.dma_start(T.tab0[0:64, :], T.tb[0:4, 0:65536]).then_inc(sem.dt0, 16)
-    Y.wait_ge(sem.dxr, 16)
-    Y.dma_start(T.tab0[64:128, :], T.tb[4:8, 0:65536]).then_inc(sem.dt0, 16)
+    def first(kind, c):
+        for w in " ".join((GO, VE, VO, "x01 t01 s01")).split():
+            if w[0] == kind and int(w[1]) <= c < int(w[2]):
+                return int(w[1])
 
-    lax = {"allow_small_or_imprecise_dtypes": True}
-    g.iota(T.pcol[:], [[1, 1]], 0, 1).then_inc(sem.iop, 1)
-    g.iota(T.diff[:], [[1, 128]], 0, -1, **lax).then_inc(sem.iod, 1)
-    g.iota(T.iotl[:], [[16, 2], [32, 8], [1, 16]], 0, 0, **lax).then_inc(sem.iol, 1)
-    g.iota(T.iotn[:], [[1, 128]], 0, 0, **lax).then_inc(sem.ion, 1)
+    starts = sorted(NCH * int(w[1]) + int(w[2]) for w in PO.split() if w[0] == "a") + [2 * NCH]
+    head = [max(s for s in starts if s <= k) for k in range(2 * NCH)]
 
-    def masks(i):
-        g.affine_select(T.lm[:, 512 * i:512 * i + 512], T.ones[:], [[1000, 4], [-16, 8], [-1001, 16]], OP.is_equal, 0.0,
-                        4000 * i, 1).then_inc(sem.lmg, 1)
+    def cast_x(e, c0, c1):
+        for c in range(c0, min(c1, last)):
+            e.wait_ge(sem["dx%d" % c], 32 if c else 16)
+        for gt in range(2):
+            if c0 == 0 and gt:
+                e.wait_ge(sem.dxs, 16)
+            out, src = T.xb[:, c0 * CS + gt:c1 * CS:2], T.xi[:, 512 * gt + half * c0:512 * gt + half * c1]
+            if e is g:
+                m = g.affine_select(out, src, [[0, half * (c1 - c0)]], OP.is_equal, 0.0, 0, 0)
+            else:
+                m = V.tensor_copy(out, src)
+            m.then_inc(sem["cv%d" % c0], 1)
 
-    def send(l, c):
-        g.wait_ge(sem["%s%d" % ("sc" if l else "ce", c)], 1)
-        a = own + c * CS
-        bcast(cb[l][:, a:a + CS], cb[l][:, a:a + CS], "%s%d" % ("bc" if l else "ac", c))
+    def turn_x(c0, c1):
+        for c in range(c0, c1):
+            V.wait_ge(sem["cv%d" % first("x", c)], 2)
+        V.transpose(T.c0[:, own + c0 * CS:own + c1 * CS], T.xb[:, c0 * CS:c1 * CS]).then_inc(sem["tr%d" % c0], 1)
 
-    g.wait_ge(sem.dgv, 16)
-    bcast(T.gs[:], T.gl[:, 4 * rank:4 * rank + 4], "agv")
-    send(0, 0)
-    g.wait_ge(sem.von, 1)
-    masks(0)
-    send(0, 1)
-    masks(1)
-    send(0, 2)
-    masks(2)
-    masks(3)
-    send(0, 3)
-    g.affine_select(T.rm[:], T.ones[:, 0:128], [[-1, 16], [-16, 8]], OP.is_equal, 0.0, 0, 1).then_inc(sem.rmg, 1)
-    for c in range(NCH):
-        send(1, c)
-    g.wait_ge(sem.loc, ne * (1 + 2 * NCH))
+    def send(l, c0, c1):
+        for c in range(c0, c1):
+            g.wait_ge(sem["sc%d" % c if l else "tr%d" % first("t", c)], 1)
+        piece = cb[l][:, own + c0 * CS:own + c1 * CS]
+        write(piece, piece, "%s%d" % ("bc" if l else "ac", c0), engs)
 
-    def onehot_wires(l, i):
-        k = 2 * l + i
-        V.tensor_scalar(T.vt[:, 256 * k:256 * k + 256], T.iotl[:], T.wf[:, k:k + 1], 64.0 if i == 0 else 1.0,
-                        OP.is_equal, OP.mult).then_inc(sem["vvt%d" % l], 1)
+    def copy(e, out, in_):
+        return V.tensor_copy(out, in_) if e is V else S.activation(out, in_, ACT.Copy)
 
     def onehot_give(l):
         for k in (2 * l, 2 * l + 1):
-            V.tensor_scalar(T.gt[:, 128 * k:128 * k + 128], T.iotn[:], T.giv[:, k:k + 1], None, OP.is_equal).then_inc(sem["vgt%d" % l], 1)
-
-    def fix(c, halves=(0, 1)):
-        P.wait_ge(sem["tr%d" % min(c, 2)], 1 if c else 8)
-        if c == 0:
-            P.wait_ge(sem.vpm, 4)
-        if c >= 2:
-            P.wait_ge(sem["ce%d" % (c - 2)], 1)
-        for h in halves:
-            for bp in range(8 if c else 1):
-                for g2 in range(2):
-                    k = 2 * g2 + h
-                    if c:
-                        i0 = c * CS + 32 * bp + 16 * g2
-                        o, i = psf[c % 2][:, 128 * h + bp:128 * h + 128:8], T.yt[:, i0:i0 + 16]
-                    else:
-                        o, i = psf[0][:, 128 * h:128 * h + 128], T.yt[:, 128 * g2:128 * g2 + 128]
-                    m = P.matmul(o, T.pm[:, 128 * k:128 * k + 128], i, g2 == 0, g2 == 1)
-            m.then_inc(sem["pf%d" % c], 1)
+            V.tensor_scalar(T.gt[:, 128 * k:128 * k + 128], T.iotn[:, 128 * l:128 * l + 128], T.giv[:, k:k + 1], None,
+                            OP.is_equal).then_inc(sem["vgt%d" % l], 1)
 
     def compose_v(l):
         P.wait_ge(sem["vvt%d" % l], 2)
@@ -162,242 +134,281 @@ def rank_program(g, core, T, topo):
                     m.then_inc(sem["pv%d" % l], 1)
 
     def w_part(l, q, kh):
-        a = 128 * q if l else 0
-        return P.matmul(psw[l][q][:, a:a + 128],
-                        T.gt[32 * q:32 * q + 32, (2 * l + kh) * 128:(2 * l + kh) * 128 + 128],
-                        T.vb[32 * q:32 * q + 32, l * 256 + 128 * kh:l * 256 + 128 * kh + 128], kh == 0, kh == 1)
+        r = slice(32 * q, 32 * q + 32)
+        lhs = T.gto[r, 128 * kh:128 * kh + 128] if (l, q) == (0, rank) else T.gt[r, (2 * l + kh) * 128:(2 * l + kh) * 128 + 128]
+        i = qs.index(q)
+        out = [B[4][:, 0:128], B[4][:, 128:256], B[7][:, 0:128], B[rank][:, 0:128]][i] if l else B[q][:, 0:128]
+        return P.matmul(out, lhs, T.vb[r, l * 256 + 128 * kh:l * 256 + 128 * kh + 128], kh == 0, kh == 1)
 
-    def compose_w0():
-        P.wait_ge(sem.sv0, 1)
+    def compose_w0(some):
         for kh in range(2):
-            P.wait_ge(sem.vgt0, kh + 1)
-            for q in range(4):
+            P.wait_ge(sem.vgto if some == [rank] else sem.vgt0, kh + 1)
+            for q in some:
                 m = w_part(0, q, kh)
                 if kh:
-                    m.then_inc(sem["pwv" if q < 3 else "pws"], 1)
+                    m.then_inc(sem["pw0%d" % q], 1)
 
-    def compose_w1():
+    def compose_w1(a, b):
         P.wait_ge(sem.vgt1, 2)
         P.wait_ge(sem.sv1, 1)
-        for q in range(4):
-            if q:
-                P.wait_ge(sem.pw1, q)
-            w_part(1, q, 0)
-            w_part(1, q, 1).then_inc(sem.pw1, 1)
+        P.wait_ge(sem["sw0%d" % rank], 1)
+        for i in (1, 2, 3, 0)[a:b]:
+            if i == 0:
+                P.wait_ge(sem.pw1, 1)
+            w_part(1, qs[i], 0)
+            w_part(1, qs[i], 1).then_inc(sem.pw1, 1)
 
-    def addresses(l, c):
-        P.wait_ge(sem["%s%d" % ("ce" if l == 0 else "sc", c)], 1)
-        P.wait_ge(sem["%s%d" % ("ac" if l == 0 else "bc", c)], ne * n_oth)
-        if c == 0:
-            P.wait_ge(sem.sw1 if l else sem.sv1, 1)
-        k = l * NCH + c - 2
-        if k >= 0:
-            P.wait_ge(sem["ea%d%d" % (k // NCH, k % NCH)], 2)
-        for q in range(4):
-            if l == 0 and c == 0:
-                P.wait_ge(sem.swv if q < 3 else sem.sws, q + 1 if q < 3 else 1)
-            m = P.matmul(psa[c % 2][:, 0:CS], T.w[:, (4 * l + q) * 128:(4 * l + q) * 128 + 128],
-                         cb[l][:, q * 1024 + c * CS:q * 1024 + (c + 1) * CS], q == 0, q == 3)
-        m.then_inc(sem["pa%d%d" % (l, c)], 1)
+    def w_out(e, q):
+        e.wait_ge(sem["pw0%d" % q], 1)
+        i = qs.index(q)
+        copy(e, T.w[:, 128 * i:128 * i + 128], B[q][:, 0:128]).then_inc(sem["sw0%d" % q], 1)
+
+    def w1_out(e, j0, j1):
+        for n, a, b, bank in ((2, 2, 3, B[7]), (3, 3, 4, B[rank]), (4, 0, 2, B[4]))[j0:j1]:
+            e.wait_ge(sem.pw1, n)
+            copy(e, T.w[:, 512 + 128 * a:512 + 128 * b], bank[:, 0:128 * (b - a)]).then_inc(sem.sw1, 1)
 
     def gpos(l, c, h):
-        if l == 0 or c < NCH - 1:
-            nv = SPL[l][c]
-            return (c * CS + nv, (c + 1) * CS) if h else (c * CS, c * CS + nv)
-        o = (NCH - 1) * CS + 128 * h
-        return (o, o + 8 * SA) if c == NCH - 1 else (o + 8 * SA, o + 128)
+        if c < len(SPL[l]):
+            a, nv, b = c * CS, SPL[l][c], (c + 1) * CS
+            return (a + nv, b) if h else (a, a + nv)
+        return tuple(last * CS + j for j in TAIL[h][c - last])
 
-    def tile(c, h):
-        return gpos(1, c, h) if c >= NCH - 1 else (c * CS + 128 * h, c * CS + 128 * h + 128)
+    def addresses(l, c):
+        k = l * NCH + c
+        bank = B[int(BANKS[k])]
+        mine = [j for j in range(2 * NCH) if head[j] == k]
+        for j in mine:
+            P.wait_ge(sem["sc%d" % (j - NCH) if l else "tr%d" % first("t", j)], 1)
+            if j:
+                P.wait_ge(sem["bc%d" % (j - NCH) if l else "ac%d" % first("s", j)], ne * n_oth)
+        if k == 1:
+            P.wait_ge(sem.sw1, 3)
+        for j in range(k):
+            if BANKS[j] == BANKS[k] or j == 0 and bank is B[6]:
+                P.wait_ge(sem["ea%d%d" % divmod(head[j], NCH)], 2)
+        jobs = []
+        for j in mine:
+            n = [1, 1, 4, 4, 4, 4, 2, 4][j]
+            o, d, st = j % NCH * CS, (j - k) * CS, 1
+            if j in (2, 3):
+                o, st = 2 * CS + j - 2, 2
+            jobs += [(bank[:, d + i:d + CS:n], o + st * i * CS // n, o + st * (i + 1) * CS // n - st + 1, st) for i in range(n)]
+        if k == 0:
+            jobs = [(b[:, j0:j1], j0, j1, 1) for b, (j0, j1) in ((bank, gpos(0, 0, 0)), (B[6], gpos(0, 0, 1)))]
+        for i, (out, a, b, st) in enumerate(jobs):
+            for q in qs:
+                if k == 0 and i == 0:
+                    P.wait_ge(sem["sw0%d" % q], 1)
+                    if q == qs[1]:
+                        P.wait_ge(sem.ac0, ne * n_oth)
+                j = 4 * l + qs.index(q)
+                m = P.matmul(out, T.w[:, 128 * j:128 * j + 128], cb[l][:, q * 1024 + a:q * 1024 + b:st], q == qs[0], q == qs[3])
+            if k == 0 or i == len(jobs) - 1:
+                m.then_inc(sem["pa%d%d" % (l, c)], 1)
 
-    def pick(l, c):
-        if c == 0:
-            if l:
-                P.wait_ge(sem.rmg, 1)
+    def pick(l, c, *halves):
+        tail = l == 1 and c >= last
+        k = l * NCH + c
+        bank = psc[k]
+        if k == 0:
+            P.wait_ge(sem.zmg, 1)
+        for j in range(k):
+            if psc[j] is bank:
+                P.wait_ge(sem["sc%d" % j if j < NCH else "sy%d" % (j - NCH)], 1)
+        for h in halves or (0, 1):
+            if tail:
+                l0, l1, form, _ = OUT[c - last]
+                for e in range(2):
+                    for i, (j0, j1) in enumerate(TAIL[e]):
+                        if j0 < 16 * l1 and j1 > 16 * l0:
+                            P.wait_ge(sem["%s1%d" % (("gv", "gs")[e], last + i)], 1)
             else:
-                P.wait_ge(sem.lmg, 4)
-        k = l * NCH + c - 2
-        if k >= 0:
-            P.wait_ge(sem["%s%d" % ("sc" if k < NCH else "sy", k % NCH)], 1)
-        for h in range(2):
-            P.wait_ge(sem["%s%d%d" % ("gs" if h else "gv", l, c)], 1)
-            j0, j1 = tile(c, h) if l else gpos(0, c, h)
-            if l and h == 0 and j1 > gpos(1, c, 0)[1]:
-                P.wait_ge(sem["gs%d%d" % (l, c)], 1)
+                P.wait_ge(sem["%s%d%d" % ("gs" if h else "gv", l, c)], 1)
+                j0, j1 = gpos(l, c, h)
+                if l and j1 < c * CS + half:
+                    P.wait_ge(sem["gs%d%d" % (l, c)], 1)
             for u in range(16):
-                src = ga[l][:, 16 * j0 + u:16 * j1:16]
+                one = T.zm[:, 32 * u:32 * u + 8]
                 if l == 0:
-                    m = P.matmul(psc[c % 2][:, j0 - c * CS:j1 - c * CS], T.lm[:, 128 * u:128 * u + 128], src, u == 0, u == 15)
+                    j, z = u // 4, 32 * u - 8 * (u % 4)
+                    m = P.matmul(bank[32 * j:32 * j + 32, j0 - c * CS:j1 - c * CS], T.zm[:, z:z + 32],
+                                 ga[0][:, 16 * j0 + u:16 * j1:16], u % 4 == 0, u % 4 == 3)
+                elif not tail:
+                    a = 16 * (c * CS + half * h)
+                    m = P.matmul(bank[:, 16 * h + u:CS:32], ga[1][:, a + u:a + 16 * half:16], one, True, True)
                 else:
-                    m = P.matmul(psc[c % 2][0:j1 - j0, 16 * h + u:256:32], src, T.rm[:, 8 * u:8 * u + 8], True, True)
+                    a = 16 * last * CS
+                    if form == 0:
+                        m = P.matmul(bank[0:8 * (l1 - l0), 16 * h + u:CS:32],
+                                     ga[1][:, a + CS * l0 + 16 * h + u:a + CS * l1:32], one, True, True)
+                    elif form == 2 and u % 2 == h:
+                        m = P.matmul(bank[0:16 * (l1 - l0), u:half:16], ga[1][:, a + CS * l0 + u:a + CS * l1:16], one, True, True)
+                    elif form == 1:
+                        for s in range(l0 + h, l1, 2):
+                            p = 32 * (s - l0)
+                            m = P.matmul(bank[p:p + 8, u:CS:16], one, ga[1][:, a + CS * s + u:a + CS * (s + 1):16], True, True)
             m.then_inc(sem["pd%d%d" % (l, c)], 1)
 
-    def evac_addr(l, c):
-        V.wait_ge(sem["pa%d%d" % (l, c)], 1)
-        for a, b in (gpos(l, c, 0), gpos(l, c, 1)) if SPL[l][c] else ((c * CS, (c + 1) * CS),):
-            V.tensor_copy(off[l][:, a:b], psa[c % 2][:, a - c * CS:b - c * CS]).then_inc(sem["ea%d%d" % (l, c)], 1)
+    def evac_addr(l, c, whole):
+        k = l * NCH + c
+        a, cut, b = c * CS, gpos(l, c, 0)[1], (c + head.count(k)) * CS
+        if k == 2 * NCH - 1:
+            cut = max(cut, gpos(l, c, 1)[1])
+        for h, (j0, j1) in enumerate([(a, b)] if whole else [(a, cut), (cut, b)]):
+            V.wait_ge(sem["pa%d%d" % (l, c)], 1 + h if k == 0 else 1)
+            bank = B[6] if k == 0 and h else B[int(BANKS[k])]
+            V.tensor_copy(off[l][:, j0:j1], bank[:, j0 - a:j1 - a]).then_inc(sem["ea%d%d" % (l, c)], 1 + whole)
 
-    def gather(l, c, h):
-        q = S if h else V
-        q.wait_ge(sem["ea%d%d" % (l, min(c, NCH - 1))], 2 if h and SPL[l][min(c, NCH - 1)] else 1)
+    def gather(e, l, c):
+        h, k = int(e is S), l * NCH + min(c, last)
+        early = (h == 0 if c < len(SPL[l]) else c == last) and "a%d%d" % (l, c) in VO
+        e.wait_ge(sem["ea%d%d" % divmod(head[k], NCH)], 1 if early else 2)
         if c == 0:
-            q.wait_ge(sem["dt%d" % l], 16 if l else 32)
+            for w in YO.split():
+                if w[:2] == "T%d" % l:
+                    e.wait_ge(sem["dt" + w[1:3]], 16)
         j0, j1 = gpos(l, c, h)
         win = tab[l][:, 0:4096].indirect(off[l][:, j0:j1])
-        if h == 0:
-            V.tensor_copy(ga[l][:, 16 * j0:16 * j1], win).then_inc(sem["gv%d%d" % (l, c)], 1)
+        copy(e, ga[l][:, 16 * j0:16 * j1], win).then_inc(sem["%s%d%d" % ("gs" if h else "gv", l, c)], 1)
+
+    def c1_out(e, c):
+        e.wait_ge(sem["pd0%d" % c], 2)
+        copy(e, T.c1[:, own + c * CS:own + (c + 1) * CS], psc[c][:, 0:CS]).then_inc(sem["sc%d" % c], 1)
+
+    def rows(c):
+        l0, l1, form, qq = OUT[c - last] if c >= last else (0, 16, 0, "Y")
+        return l0, l1, form, qq, [8 * (l1 - l0), 32 * (l1 - l0 - 1) + 8, 16 * (l1 - l0)][form], [CS, CS, half][form]
+
+    def y_out(e, c):
+        e.wait_ge(sem["pd1%d" % c], 2)
+        n, w = rows(c)[4:]
+        copy(e, T.ys[0:n, c * CS:c * CS + w], psc[NCH + c][0:n, 0:w]).then_inc(sem["sy%d" % c], 1)
+
+    nst = [0]
+
+    def store(e, c):
+        l0, l1, form, qq, n, w = rows(c)
+        a, y0 = c * CS, min(c, last) * CS
+        if form == 1:
+            pairs = [(T.y[s:128:16, y0:y0 + CS], T.ys[32 * (s - l0):32 * (s - l0) + 8, a:a + CS]) for s in range(l0, l1)]
         else:
-            S.activation(ga[l][:, 16 * j0:16 * j1], win, ACT.Copy).then_inc(sem["gs%d%d" % (l, c)], 1)
+            pairs = [(T.y[16 * j + l0:16 * j + l1, y0:y0 + CS], T.ys[0:n, a + w // 8 * j:a + w // 8 * (j + 1)]) for j in range(8)]
+        pairs = [p for i, p in enumerate(pairs) if qq[i % len(qq)] == ("Y" if e is Y else "S")]
+        if pairs:
+            e.wait_ge(sem["sy%d" % c], 1)
+        for o, s in pairs:
+            e.dma_start(o, s).then_inc(sem.dy, 16)
+            nst[0] += 1
 
-    def s_c0(c):
-        S.wait_ge(sem["pf%d" % c], 2)
-        S.activation(T.c0[:, own + c * CS:own + (c + 1) * CS], psf[c % 2][:, 0:CS], ACT.Copy).then_inc(sem["ce%d" % c], 1)
+    def load_x(c):
+        for gt in range(2):
+            a, n = 512 * gt + half * c, 2 if c == 2 else 1
+            q, s = (S, sem.dxs) if c == 0 and gt else (Y, sem["dx%d" % c])
+            q.dma_start(T.xi[:, a:a + n * half], T.x[64 * gt:64 * gt + 64, c * CS:(c + n) * CS]).then_inc(s, 16)
 
-    def s_c1(c):
-        S.wait_ge(sem["pd0%d" % c], 2)
-        S.activation(T.c1[:, own + c * CS:own + (c + 1) * CS], psc[c % 2][:, 0:CS], ACT.Copy).then_inc(sem["sc%d" % c], 1)
+    def load_tab(l, a, b):
+        Y.dma_start(tab[l][16 * a:16 * b, :], T.tb[a:b, 65536 * l:65536 * (l + 1)]).then_inc(sem["dt%d%d" % (l, a)], 16)
 
-    def ysrc(c):
-        if c < NCH - 1:
-            return T.ys, c * CS, 128
-        return (T.ys, (NCH - 1) * CS, 8 * SA) if c == NCH - 1 else (T.yl, 0, 128 - 8 * SA)
+    def mask():
+        g.wait_ge(sem.von, 1)
+        g.affine_select(T.zm[:], T.ones[:], [[-1, 16], [1000, 4], [-16, 8]], OP.is_equal, 0.0, 0, 1).then_inc(sem.zmg, 1)
 
-    def out_y(q, c):
-        q.wait_ge(sem["pd1%d" % c], 2)
-        b, a, n = ysrc(c)
-        if q is V:
-            m = V.tensor_copy(b[0:n, a:a + CS], psc[c % 2][0:n, 0:CS])
-        else:
-            m = S.activation(b[0:n, a:a + CS], psc[c % 2][0:n, 0:CS], ACT.Copy)
-        m.then_inc(sem["sy%d" % c], 1)
+    def run(e, order):
+        for w in order.split():
+            n = [int(d) for d in w[1:]]
+            if e is P:
+                {"a": addresses, "p": pick, "w": compose_w1}[w[0]](*n)
+            elif e is Y:
+                {"l": load_x, "T": load_tab, "i": lambda k: Y.wait_ge(sem.gone, k), "e": lambda c: Y.wait_ge(sem["ea0%d" % c], 2), "p": lambda c: Y.wait_ge(sem["pa0%d" % c], 1),
+                 "x": lambda c: Y.wait_ge(sem["dx%d" % c], 32 if c else 16), "t": lambda a: Y.wait_ge(sem["dt0%d" % a], 16)}[w[0]](*n)
+            elif w[0] in "ab":
+                evac_addr(*n, int(w[0] == "b"))
+            elif w[0] == "v":
+                w_out(e, qs[n[0]])
+            elif w[0] in "tsmio":
+                {"o": onehot_give, "t": turn_x, "s": lambda a, b: send(0, a, b), "m": mask, "i": lambda: g.sem_inc(sem.gone, 1)}[w[0]](*n)
+            else:
+                {"g": gather, "c": c1_out, "y": y_out, "w": w1_out, "x": cast_x, "z": store}[w[0]](e, *n)
+
+    S.dma_start(T.gs[:], T.give[:]).then_inc(sem.dgv, 16)
+    Y.dma_start(T.wi[:], T.wires[:]).then_inc(sem.dwr, 16)
+    run(Y, YO)
+
+    lax = {"allow_small_or_imprecise_dtypes": True}
+    g.iota(T.diff[:], [[1, 128]], 0, -1, **lax).then_inc(sem.iod, 1)
+    g.iota(T.iotl[:], [[16, 2], [32, 8], [1, 16]], 0, 0, **lax).then_inc(sem.iol, 1)
+    g.wait_ge(sem.dgv, 16)
+    write(T.gs[:], T.gl[:, 4 * rank:4 * rank + 4], "agv", engs[::GDIV])
+    send(0, 0, 1)
+    run(g, GO)
+    for c in range(NCH):
+        send(1, c, c + 1)
+    g.wait_ge(sem.loc, sent[0])
 
     V.memset(T.ones[:], 1.0).then_inc(sem.von, 1)
-    V.wait_ge(sem.iop, 1)
-    V.tensor_scalar(T.kbi[:], T.pcol[:], 4, 1, OP.logical_shift_right, OP.bitwise_and).then_inc(sem.vi, 1)
-    V.wait_ge(sem.vi, 1)
-    V.tensor_copy(T.kbf[:, 1:2], T.kbi[:]).then_inc(sem.vf, 1)
-    V.tensor_scalar(T.kbf[:, 0:1], T.kbi[:], -1.0, 1.0, OP.mult, OP.add).then_inc(sem.vf, 1)
+    V.memset(T.step[:, 128:256], 16.0).then_inc(sem.vst, 1)
+    V.memset(T.step[:, 0:128:2], -63.0).then_inc(sem.vst, 1)
+    V.memset(T.step[:, 1:128:2], 64.0).then_inc(sem.vst, 1)
+    V.wait_ge(sem.vst, 1)
+    V.memset(T.step[:, 128:256:8], -111.0).then_inc(sem.vst, 1)
+    V.wait_ge(sem.von, 1)
+    V.wait_ge(sem.vst, 4)
+    for l in range(2):
+        a = slice(128 * l, 128 * l + 128)
+        V.tensor_tensor_scan(T.iotn[:, a], T.ones[:, 0:128], T.step[:, a], [63.0, 111.0][l], OP.mult, OP.add).then_inc(sem.ion, 1)
     V.wait_ge(sem.iod, 1)
     V.tensor_scalar(T.ident[:], T.diff[:], 0.0, None, OP.is_equal).then_inc(sem.vid, 1)
-    V.wait_ge(sem.vf, 2)
-    for g2 in range(2):
-        for h in range(2):
-            k = 2 * g2 + h
-            V.tensor_scalar(T.pm[:, 128 * k:128 * k + 128], T.diff[:], float(16 * (g2 - h)), T.kbf[:, h:h + 1],
-                            OP.is_equal, OP.mult).then_inc(sem.vpm, 1)
-    V.wait_ge(sem.dx0, 16)
-    for h in range(2):
-        V.tensor_copy(T.xb[:, 128 * h:128 * h + 128], T.xi[:, 128 * h:128 * h + 128]).then_inc(sem.cv0, 1)
+    r0 = slice(32 * rank, 32 * rank + 32)
     V.wait_ge(sem.dwr, 16)
-    V.tensor_copy(T.wf[:], T.wi[:]).then_inc(sem.vwf, 1)
-    for bp in range(8):
-        V.wait_ge(sem.cv0, 1 + bp // 4)
-        V.transpose(T.yt[:, bp:CS:8], T.xb[:, 32 * bp:32 * bp + 32]).then_inc(sem.tr0, 1)
+    V.tensor_scalar(T.wf[:, 4:8], T.wi[:], -1.0, None, OP.mult).then_inc(sem.vwn, 1)
+    V.tensor_copy(T.wf[:, 0:4], T.wi[:]).then_inc(sem.vwf, 1)
+    cast_x(V, 0, 1)
+    V.wait_ge(sem.dgv, 16)
+    V.tensor_copy(T.giv[r0, :], T.gs[r0, :]).then_inc(sem.vgio, 1)
+    turn_x(0, 1)
     V.wait_ge(sem.iol, 1)
     V.wait_ge(sem.vwf, 1)
-    onehot_wires(0, 0)
-    V.wait_ge(sem.dxr, 16)
-    V.tensor_copy(T.xb[:, CS:2 * CS], T.xi[:, CS:2 * CS]).then_inc(sem.cv1, 1)
-    onehot_wires(0, 1)
-    V.wait_ge(sem.cv1, 1)
-    V.transpose(T.yt[:, CS:2 * CS], T.xb[:, CS:2 * CS]).then_inc(sem.tr1, 1)
-    V.tensor_copy(T.xb[:, 2 * CS:1024], T.xi[:, 2 * CS:1024]).then_inc(sem.cv2, 1)
-    onehot_wires(1, 0)
-    onehot_wires(1, 1)
-    V.wait_ge(sem.cv2, 1)
-    V.transpose(T.yt[:, 2 * CS:1024], T.xb[:, 2 * CS:1024]).then_inc(sem.tr2, 1)
-    V.wait_ge(sem.ion, 1)
-    V.wait_ge(sem.dgv, 16)
-    V.wait_ge(sem.agv, ne * n_oth)
-    for q in range(4):
-        r0 = 32 * rank
-        src = T.gs[r0:r0 + 32, 0:4] if q == rank else T.gl[r0:r0 + 32, 4 * q:4 * q + 4]
-        V.tensor_copy(T.giv[32 * q:32 * q + 32, 0:4], src).then_inc(sem.vgiv, 1)
-    V.wait_ge(sem.vgiv, 4)
+    for i in range(2):
+        V.tensor_scalar(T.vt[:, 256 * i:256 * i + 256], T.iotl[:], T.wf[:, i:i + 1], [64.0, 1.0][i],
+                        OP.is_equal, OP.mult).then_inc(sem.vvt0, 1)
+    V.wait_ge(sem.ion, 2)
+    V.wait_ge(sem.vgio, 1)
+    for k in range(2):
+        V.tensor_scalar(T.gto[r0, 128 * k:128 * k + 128], T.iotn[r0, 0:128], T.giv[r0, k:k + 1], None,
+                        OP.is_equal).then_inc(sem.vgto, 1)
+    run(V, VE)
+    V.wait_ge(sem.agv, ng * n_oth)
+    for q in qs[1:]:
+        V.tensor_copy(T.giv[32 * q:32 * q + 32, 0:4], T.gl[r0, 4 * q:4 * q + 4]).then_inc(sem.vgiv, 1)
+    V.wait_ge(sem.vgiv, 3)
     onehot_give(0)
-    for q in range(3):
-        V.wait_ge(sem.pwv, q + 1)
-        V.tensor_copy(T.w[:, 128 * q:128 * q + 128], psw[0][q][:, 0:128]).then_inc(sem.swv, 1)
-    onehot_give(1)
-    for c in range(NCH):
-        evac_addr(0, c)
-        gather(0, c, 0)
-    for c in range(NCH):
-        evac_addr(1, c)
-        if c == NCH - 1:
-            out_y(V, 1)
-        gather(1, c, 0)
-    out_y(V, 2)
-    gather(1, 4, 0)
-    out_y(V, 3)
-    out_y(V, 4)
+    run(V, VO)
 
-    s_c0(0)
+    S.wait_ge(sem.iol, 1)
+    S.wait_ge(sem.vwn, 1)
+    for i in range(2):
+        S.activation(T.vt[:, 512 + 256 * i:768 + 256 * i], T.iotl[:], ACT.Abs, bias=T.wf[:, 6 + i:7 + i]).then_inc(sem.sab, 1)
+    for i in range(2):
+        S.wait_ge(sem.sab, i + 1)
+        a, top = T.vt[:, 512 + 256 * i:768 + 256 * i], [64.0, 1.0][i]
+        S.activation(a, a, ACT.Relu, bias=top, scale=-top).then_inc(sem.vvt1, 1)
     S.wait_ge(sem.pv0, 2)
-    S.activation(T.vb[:, 0:256], psv[0][:, 0:256], ACT.Copy).then_inc(sem.sv0, 1)
-    s_c0(1)
+    copy(S, T.vb[:, 0:256], psv[0][:, 0:256]).then_inc(sem.sv0, 1)
+    w_out(S, rank)
     S.wait_ge(sem.pv1, 2)
-    S.activation(T.vb[:, 256:512], psv[1][:, 0:256], ACT.Copy).then_inc(sem.sv1, 1)
-    S.wait_ge(sem.pws, 1)
-    S.activation(T.w[:, 384:512], psw[0][3][:, 0:128], ACT.Copy).then_inc(sem.sws, 1)
-    s_c0(2)
-    gather(0, 0, 1)
-    s_c0(3)
-    S.wait_ge(sem.pw1, 4)
-    S.activation(T.w[:, 512:1024], T.psw[:], ACT.Copy).then_inc(sem.sw1, 1)
-    gather(0, 1, 1)
-    s_c1(0)
-    gather(0, 2, 1)
-    s_c1(1)
-    gather(0, 3, 1)
-    s_c1(2)
-    gather(1, 0, 1)
-    s_c1(3)
-    gather(1, 1, 1)
-    out_y(S, 0)
-    gather(1, 2, 1)
-    gather(1, 3, 1)
-    gather(1, 4, 1)
+    copy(S, T.vb[:, 256:512], psv[1][:, 0:256]).then_inc(sem.sv1, 1)
+    w_out(S, qs[2])
+    run(S, SO)
 
     P.wait_ge(sem.vid, 1)
-    fix(0)
     compose_v(0)
-    fix(1)
+    P.wait_ge(sem.sv0, 1)
+    compose_w0([rank])
     compose_v(1)
-    fix(2, (0,))
-    compose_w0()
-    fix(2, (1,))
-    addresses(0, 0)
-    fix(3)
-    compose_w1()
-    addresses(0, 1)
-    pick(0, 0)
-    addresses(0, 2)
-    pick(0, 1)
-    addresses(0, 3)
-    pick(0, 2)
-    addresses(1, 0)
-    pick(0, 3)
-    addresses(1, 1)
-    pick(1, 0)
-    addresses(1, 2)
-    pick(1, 1)
-    addresses(1, 3)
-    pick(1, 2)
-    pick(1, 3)
-    pick(1, 4)
+    compose_w0(qs[1:])
+    run(P, PO)
 
-    Y.wait_ge(sem.ea00, 2)
-    Y.dma_start(T.tab1[:], T.tb[:, 65536:131072]).then_inc(sem.dt1, 16)
-    for c in range(NCH + 1):
-        last = c >= NCH - 1
-        Y.wait_ge(sem["sy%d" % c], 1)
-        if last:
-            S.wait_ge(sem["sy%d" % c], 1)
-        b, a, n = ysrc(c)
-        cc = min(c, NCH - 1)
-        for gg in range(8):
-            q = S if last and gg % 2 else Y
-            r0 = 16 * gg + (SA if c == NCH else 0)
-            q.dma_start(T.y[r0:r0 + n // 8, cc * CS:(cc + 1) * CS], b[0:n, a + 32 * gg:a + 32 * gg + 32]).then_inc(sem.dy, 16)
-    Y.wait_ge(sem.dy, 16 * 8 * (NCH + 1))
+    for c in range(last + len(OUT)):
+        store(Y, c)
+    Y.wait_ge(sem.dy, 16 * nst[0])

from concourse.bass import DstId, RemoteDMATransfer
from concourse.mybir import AluOpType as OP, ActivationFunctionType as ACT

NCH = 4
CS = 256
SPL = [[122, 118, 136, 128], [128, 128, 128]]
TAIL = [[(0, 86), (160, 210)], [(86, 160), (210, 256)]]
OUT = [(0, 10, 0, "YS"), (10, 16, 2, "YS")]
GDIV = 2
YO = "l0 l1 l2 T003 i1 T038 p1 T108"
GO = "i x24 s12 m s24"
VE = "x12 t12"
VO = "o1 t24 v1 v3 a00 g00 b01 b02 g01 g02 a03 g03 a10 g10 a11 g11 a12 g12 a13 g13 g14 y4"
SO = "w03 g00 g01 c0 g02 c1 g03 c2 g10 c3 g11 y0 g12 y1 g13 y2 g14 y3 z3 z4"
PO = "w04 a00 a01 a02 p00 a03 p01 p020 a10 p021 p030 a11 p031 p10 a12 p11 a13 p12 p13 p14"
BANKS = "57567567"

SCRATCH = {
    "xi": ("sbuf", [128, 1024], "int32"),
    "xb": ("sbuf", [128, 1024], "bfloat16"),
    "gs": ("sbuf", [128, 4], "int32"),
    "gl": ("sbuf", [128, 16], "int32"),
    "giv": ("sbuf", [128, 4], "float32"),
    "wi": ("sbuf", [128, 4], "int32"),
    "wf": ("sbuf", [128, 8], "float32"),
    "ones": ("sbuf", [128, 512], "bfloat16"),
    "step": ("sbuf", [128, 256], "bfloat16"),
    "diff": ("sbuf", [128, 128], "bfloat16"),
    "iotn": ("sbuf", [128, 256], "bfloat16"),
    "iotl": ("sbuf", [128, 256], "bfloat16"),
    "ident": ("sbuf", [128, 128], "bfloat16"),
    "zm": ("sbuf", [128, 512], "bfloat16"),
    "vt": ("sbuf", [128, 1024], "bfloat16"),
    "vb": ("sbuf", [128, 512], "bfloat16"),
    "gt": ("sbuf", [128, 512], "bfloat16"),
    "gto": ("sbuf", [128, 256], "bfloat16"),
    "w": ("sbuf", [128, 1024], "bfloat16"),
    "c0": ("sbuf", [128, 4096], "bfloat16"),
    "c1": ("sbuf", [128, 4096], "bfloat16"),
    "tab0": ("sbuf", [128, 4096], "bfloat16"),
    "tab1": ("sbuf", [128, 4096], "bfloat16"),
    "off0": ("sbuf", [128, 1024], "uint16"),
    "off1": ("sbuf", [128, 1024], "uint16"),
    "ga0": ("sbuf", [128, 16384], "bfloat16"),
    "ga1": ("sbuf", [128, 16384], "bfloat16"),
    "ys": ("sbuf", [128, 1792], "float32"),
}
SCRATCH.update({"b%d" % i: ("psum", [128, 512], "float32") for i in range(8)})
SEMAPHORES = (["dgv", "dwr", "dxs", "dy", "iod", "iol", "ion", "von", "vst", "vwn", "sab", "zmg", "vid", "vwf",
               "vvt0", "vvt1", "vgio", "vgto", "vgiv", "vgt0", "vgt1", "pv0", "pv1", "sv0", "sv1", "pw1", "sw1", "agv",
               "loc", "gone"]
              + ["%s%d" % (a, c) for c in range(NCH) for a in ("dx", "cv", "tr", "ac", "pw0", "sw0", "bc", "sc")]
              + ["%s%d%d" % (a, l, c) for l in range(2) for c in range(NCH) for a in ("pa", "ea")]
              + ["%s%d%d" % (a, l, c) for l in range(2) for c in range(NCH + 4 * l) for a in ("gv", "gs", "pd")]
              + ["sy%d" % c for c in range(NCH + 3)] + ["dt" + w[1:3] for w in YO.split() if w[0] == "T"])


def rank_program(g, core, T, topo):
    rank = T.rank_of(core)
    if rank is None:
        return
    V, S, P, Y = g.vector, g.scalar, g.tensor, g.sync
    sem = T.sem
    others = [c for c in T.cores if c != core]
    n_oth = len(others)
    engs = topo.engines(core, others[0])
    for c in others:
        engs = [e for e in engs if e in topo.engines(core, c)]
    ne = len(engs)
    ng = ne // GDIV
    ids = [DstId(rid=topo.addr(c)[0], pnc=topo.addr(c)[1]) for c in others]
    sent = [0]

    def write(src, dst, name, engines):
        g.remote_dma_fused([RemoteDMATransfer(dst_ids=ids, dma_engine_mask=sum(1 << e for e in engines), remote_sem=sem[name],
                                              srcs=[src], dsts=[dst] * n_oth)], local_sem=sem.loc)
        sent[0] += len(engines)

    own = rank * 1024
    B = [T["b%d" % i] for i in range(8)]
    cb, tab, off, ga = [T.c0, T.c1], [T.tab0, T.tab1], [T.off0, T.off1], [T.ga0, T.ga1]
    qs = [rank] + [q for q in range(4) if q != rank]
    psv, psw1 = [B[4], B[7]], B[4]
    last, half = NCH - 1, CS // 2
    psc = [B[0], B[1], B[0], B[1], B[2], B[3], B[2], B[0], B[1], B[4], B[3]]

    def first(kind, c):
        for w in " ".join((GO, VE, VO, "x01 t01 s01")).split():
            if w[0] == kind and int(w[1]) <= c < int(w[2]):
                return int(w[1])

    starts = sorted(NCH * int(w[1]) + int(w[2]) for w in PO.split() if w[0] == "a") + [2 * NCH]
    head = [max(s for s in starts if s <= k) for k in range(2 * NCH)]

    def cast_x(e, c0, c1):
        for c in range(c0, min(c1, last)):
            e.wait_ge(sem["dx%d" % c], 32 if c else 16)
        for gt in range(2):
            if c0 == 0 and gt:
                e.wait_ge(sem.dxs, 16)
            out, src = T.xb[:, c0 * CS + gt:c1 * CS:2], T.xi[:, 512 * gt + half * c0:512 * gt + half * c1]
            if e is g:
                m = g.affine_select(out, src, [[0, half * (c1 - c0)]], OP.is_equal, 0.0, 0, 0)
            else:
                m = V.tensor_copy(out, src)
            m.then_inc(sem["cv%d" % c0], 1)

    def turn_x(c0, c1):
        for c in range(c0, c1):
            V.wait_ge(sem["cv%d" % first("x", c)], 2)
        V.transpose(T.c0[:, own + c0 * CS:own + c1 * CS], T.xb[:, c0 * CS:c1 * CS]).then_inc(sem["tr%d" % c0], 1)

    def send(l, c0, c1):
        for c in range(c0, c1):
            g.wait_ge(sem["sc%d" % c if l else "tr%d" % first("t", c)], 1)
        piece = cb[l][:, own + c0 * CS:own + c1 * CS]
        write(piece, piece, "%s%d" % ("bc" if l else "ac", c0), engs)

    def copy(e, out, in_):
        return V.tensor_copy(out, in_) if e is V else S.activation(out, in_, ACT.Copy)

    def onehot_give(l):
        for k in (2 * l, 2 * l + 1):
            V.tensor_scalar(T.gt[:, 128 * k:128 * k + 128], T.iotn[:, 128 * l:128 * l + 128], T.giv[:, k:k + 1], None,
                            OP.is_equal).then_inc(sem["vgt%d" % l], 1)

    def compose_v(l):
        P.wait_ge(sem["vvt%d" % l], 2)
        for kh in range(2):
            for i in range(2):
                a = (2 * l + i) * 256 + 128 * kh
                m = P.matmul(psv[l][:, 128 * kh:128 * kh + 128], T.vt[:, a:a + 128], T.ident[:], i == 0, i == 1)
                if i == 1:
                    m.then_inc(sem["pv%d" % l], 1)

    def w_part(l, q, kh):
        r = slice(32 * q, 32 * q + 32)
        lhs = T.gto[r, 128 * kh:128 * kh + 128] if (l, q) == (0, rank) else T.gt[r, (2 * l + kh) * 128:(2 * l + kh) * 128 + 128]
        i = qs.index(q)
        out = [B[4][:, 0:128], B[4][:, 128:256], B[7][:, 0:128], B[rank][:, 0:128]][i] if l else B[q][:, 0:128]
        return P.matmul(out, lhs, T.vb[r, l * 256 + 128 * kh:l * 256 + 128 * kh + 128], kh == 0, kh == 1)

    def compose_w0(some):
        for kh in range(2):
            P.wait_ge(sem.vgto if some == [rank] else sem.vgt0, kh + 1)
            for q in some:
                m = w_part(0, q, kh)
                if kh:
                    m.then_inc(sem["pw0%d" % q], 1)

    def compose_w1(a, b):
        P.wait_ge(sem.vgt1, 2)
        P.wait_ge(sem.sv1, 1)
        P.wait_ge(sem["sw0%d" % rank], 1)
        for i in (1, 2, 3, 0)[a:b]:
            if i == 0:
                P.wait_ge(sem.pw1, 1)
            w_part(1, qs[i], 0)
            w_part(1, qs[i], 1).then_inc(sem.pw1, 1)

    def w_out(e, q):
        e.wait_ge(sem["pw0%d" % q], 1)
        i = qs.index(q)
        copy(e, T.w[:, 128 * i:128 * i + 128], B[q][:, 0:128]).then_inc(sem["sw0%d" % q], 1)

    def w1_out(e, j0, j1):
        for n, a, b, bank in ((2, 2, 3, B[7]), (3, 3, 4, B[rank]), (4, 0, 2, B[4]))[j0:j1]:
            e.wait_ge(sem.pw1, n)
            copy(e, T.w[:, 512 + 128 * a:512 + 128 * b], bank[:, 0:128 * (b - a)]).then_inc(sem.sw1, 1)

    def gpos(l, c, h):
        if c < len(SPL[l]):
            a, nv, b = c * CS, SPL[l][c], (c + 1) * CS
            return (a + nv, b) if h else (a, a + nv)
        return tuple(last * CS + j for j in TAIL[h][c - last])

    def addresses(l, c):
        k = l * NCH + c
        bank = B[int(BANKS[k])]
        mine = [j for j in range(2 * NCH) if head[j] == k]
        for j in mine:
            P.wait_ge(sem["sc%d" % (j - NCH) if l else "tr%d" % first("t", j)], 1)
            if j:
                P.wait_ge(sem["bc%d" % (j - NCH) if l else "ac%d" % first("s", j)], ne * n_oth)
        if k == 1:
            P.wait_ge(sem.sw1, 3)
        for j in range(k):
            if BANKS[j] == BANKS[k] or j == 0 and bank is B[6]:
                P.wait_ge(sem["ea%d%d" % divmod(head[j], NCH)], 2)
        jobs = []
        for j in mine:
            n = [1, 1, 4, 4, 4, 4, 2, 4][j]
            o, d, st = j % NCH * CS, (j - k) * CS, 1
            if j in (2, 3):
                o, st = 2 * CS + j - 2, 2
            jobs += [(bank[:, d + i:d + CS:n], o + st * i * CS // n, o + st * (i + 1) * CS // n - st + 1, st) for i in range(n)]
        if k == 0:
            jobs = [(b[:, j0:j1], j0, j1, 1) for b, (j0, j1) in ((bank, gpos(0, 0, 0)), (B[6], gpos(0, 0, 1)))]
        for i, (out, a, b, st) in enumerate(jobs):
            for q in qs:
                if k == 0 and i == 0:
                    P.wait_ge(sem["sw0%d" % q], 1)
                    if q == qs[1]:
                        P.wait_ge(sem.ac0, ne * n_oth)
                j = 4 * l + qs.index(q)
                m = P.matmul(out, T.w[:, 128 * j:128 * j + 128], cb[l][:, q * 1024 + a:q * 1024 + b:st], q == qs[0], q == qs[3])
            if k == 0 or i == len(jobs) - 1:
                m.then_inc(sem["pa%d%d" % (l, c)], 1)

    def pick(l, c, *halves):
        tail = l == 1 and c >= last
        k = l * NCH + c
        bank = psc[k]
        if k == 0:
            P.wait_ge(sem.zmg, 1)
        for j in range(k):
            if psc[j] is bank:
                P.wait_ge(sem["sc%d" % j if j < NCH else "sy%d" % (j - NCH)], 1)
        for h in halves or (0, 1):
            if tail:
                l0, l1, form, _ = OUT[c - last]
                for e in range(2):
                    for i, (j0, j1) in enumerate(TAIL[e]):
                        if j0 < 16 * l1 and j1 > 16 * l0:
                            P.wait_ge(sem["%s1%d" % (("gv", "gs")[e], last + i)], 1)
            else:
                P.wait_ge(sem["%s%d%d" % ("gs" if h else "gv", l, c)], 1)
                j0, j1 = gpos(l, c, h)
                if l and j1 < c * CS + half:
                    P.wait_ge(sem["gs%d%d" % (l, c)], 1)
            for u in range(16):
                one = T.zm[:, 32 * u:32 * u + 8]
                if l == 0:
                    j, z = u // 4, 32 * u - 8 * (u % 4)
                    m = P.matmul(bank[32 * j:32 * j + 32, j0 - c * CS:j1 - c * CS], T.zm[:, z:z + 32],
                                 ga[0][:, 16 * j0 + u:16 * j1:16], u % 4 == 0, u % 4 == 3)
                elif not tail:
                    a = 16 * (c * CS + half * h)
                    m = P.matmul(bank[:, 16 * h + u:CS:32], ga[1][:, a + u:a + 16 * half:16], one, True, True)
                else:
                    a = 16 * last * CS
                    if form == 0:
                        m = P.matmul(bank[0:8 * (l1 - l0), 16 * h + u:CS:32],
                                     ga[1][:, a + CS * l0 + 16 * h + u:a + CS * l1:32], one, True, True)
                    elif form == 2 and u % 2 == h:
                        m = P.matmul(bank[0:16 * (l1 - l0), u:half:16], ga[1][:, a + CS * l0 + u:a + CS * l1:16], one, True, True)
                    elif form == 1:
                        for s in range(l0 + h, l1, 2):
                            p = 32 * (s - l0)
                            m = P.matmul(bank[p:p + 8, u:CS:16], one, ga[1][:, a + CS * s + u:a + CS * (s + 1):16], True, True)
            m.then_inc(sem["pd%d%d" % (l, c)], 1)

    def evac_addr(l, c, whole):
        k = l * NCH + c
        a, cut, b = c * CS, gpos(l, c, 0)[1], (c + head.count(k)) * CS
        if k == 2 * NCH - 1:
            cut = max(cut, gpos(l, c, 1)[1])
        for h, (j0, j1) in enumerate([(a, b)] if whole else [(a, cut), (cut, b)]):
            V.wait_ge(sem["pa%d%d" % (l, c)], 1 + h if k == 0 else 1)
            bank = B[6] if k == 0 and h else B[int(BANKS[k])]
            V.tensor_copy(off[l][:, j0:j1], bank[:, j0 - a:j1 - a]).then_inc(sem["ea%d%d" % (l, c)], 1 + whole)

    def gather(e, l, c):
        h, k = int(e is S), l * NCH + min(c, last)
        early = (h == 0 if c < len(SPL[l]) else c == last) and "a%d%d" % (l, c) in VO
        e.wait_ge(sem["ea%d%d" % divmod(head[k], NCH)], 1 if early else 2)
        if c == 0:
            for w in YO.split():
                if w[:2] == "T%d" % l:
                    e.wait_ge(sem["dt" + w[1:3]], 16)
        j0, j1 = gpos(l, c, h)
        win = tab[l][:, 0:4096].indirect(off[l][:, j0:j1])
        copy(e, ga[l][:, 16 * j0:16 * j1], win).then_inc(sem["%s%d%d" % ("gs" if h else "gv", l, c)], 1)

    def c1_out(e, c):
        e.wait_ge(sem["pd0%d" % c], 2)
        copy(e, T.c1[:, own + c * CS:own + (c + 1) * CS], psc[c][:, 0:CS]).then_inc(sem["sc%d" % c], 1)

    def rows(c):
        l0, l1, form, qq = OUT[c - last] if c >= last else (0, 16, 0, "Y")
        return l0, l1, form, qq, [8 * (l1 - l0), 32 * (l1 - l0 - 1) + 8, 16 * (l1 - l0)][form], [CS, CS, half][form]

    def y_out(e, c):
        e.wait_ge(sem["pd1%d" % c], 2)
        n, w = rows(c)[4:]
        copy(e, T.ys[0:n, c * CS:c * CS + w], psc[NCH + c][0:n, 0:w]).then_inc(sem["sy%d" % c], 1)

    nst = [0]

    def store(e, c):
        l0, l1, form, qq, n, w = rows(c)
        a, y0 = c * CS, min(c, last) * CS
        if form == 1:
            pairs = [(T.y[s:128:16, y0:y0 + CS], T.ys[32 * (s - l0):32 * (s - l0) + 8, a:a + CS]) for s in range(l0, l1)]
        else:
            pairs = [(T.y[16 * j + l0:16 * j + l1, y0:y0 + CS], T.ys[0:n, a + w // 8 * j:a + w // 8 * (j + 1)]) for j in range(8)]
        pairs = [p for i, p in enumerate(pairs) if qq[i % len(qq)] == ("Y" if e is Y else "S")]
        if pairs:
            e.wait_ge(sem["sy%d" % c], 1)
        for o, s in pairs:
            e.dma_start(o, s).then_inc(sem.dy, 16)
            nst[0] += 1

    def load_x(c):
        for gt in range(2):
            a, n = 512 * gt + half * c, 2 if c == 2 else 1
            q, s = (S, sem.dxs) if c == 0 and gt else (Y, sem["dx%d" % c])
            q.dma_start(T.xi[:, a:a + n * half], T.x[64 * gt:64 * gt + 64, c * CS:(c + n) * CS]).then_inc(s, 16)

    def load_tab(l, a, b):
        Y.dma_start(tab[l][16 * a:16 * b, :], T.tb[a:b, 65536 * l:65536 * (l + 1)]).then_inc(sem["dt%d%d" % (l, a)], 16)

    def mask():
        g.wait_ge(sem.von, 1)
        g.affine_select(T.zm[:], T.ones[:], [[-1, 16], [1000, 4], [-16, 8]], OP.is_equal, 0.0, 0, 1).then_inc(sem.zmg, 1)

    def run(e, order):
        for w in order.split():
            n = [int(d) for d in w[1:]]
            if e is P:
                {"a": addresses, "p": pick, "w": compose_w1}[w[0]](*n)
            elif e is Y:
                {"l": load_x, "T": load_tab, "i": lambda k: Y.wait_ge(sem.gone, k), "e": lambda c: Y.wait_ge(sem["ea0%d" % c], 2), "p": lambda c: Y.wait_ge(sem["pa0%d" % c], 1),
                 "x": lambda c: Y.wait_ge(sem["dx%d" % c], 32 if c else 16), "t": lambda a: Y.wait_ge(sem["dt0%d" % a], 16)}[w[0]](*n)
            elif w[0] in "ab":
                evac_addr(*n, int(w[0] == "b"))
            elif w[0] == "v":
                w_out(e, qs[n[0]])
            elif w[0] in "tsmio":
                {"o": onehot_give, "t": turn_x, "s": lambda a, b: send(0, a, b), "m": mask, "i": lambda: g.sem_inc(sem.gone, 1)}[w[0]](*n)
            else:
                {"g": gather, "c": c1_out, "y": y_out, "w": w1_out, "x": cast_x, "z": store}[w[0]](e, *n)

    S.dma_start(T.gs[:], T.give[:]).then_inc(sem.dgv, 16)
    Y.dma_start(T.wi[:], T.wires[:]).then_inc(sem.dwr, 16)
    run(Y, YO)

    lax = {"allow_small_or_imprecise_dtypes": True}
    g.iota(T.diff[:], [[1, 128]], 0, -1, **lax).then_inc(sem.iod, 1)
    g.iota(T.iotl[:], [[16, 2], [32, 8], [1, 16]], 0, 0, **lax).then_inc(sem.iol, 1)
    g.wait_ge(sem.dgv, 16)
    write(T.gs[:], T.gl[:, 4 * rank:4 * rank + 4], "agv", engs[::GDIV])
    send(0, 0, 1)
    run(g, GO)
    for c in range(NCH):
        send(1, c, c + 1)
    g.wait_ge(sem.loc, sent[0])

    V.memset(T.ones[:], 1.0).then_inc(sem.von, 1)
    V.memset(T.step[:, 128:256], 16.0).then_inc(sem.vst, 1)
    V.memset(T.step[:, 0:128:2], -63.0).then_inc(sem.vst, 1)
    V.memset(T.step[:, 1:128:2], 64.0).then_inc(sem.vst, 1)
    V.wait_ge(sem.vst, 1)
    V.memset(T.step[:, 128:256:8], -111.0).then_inc(sem.vst, 1)
    V.wait_ge(sem.von, 1)
    V.wait_ge(sem.vst, 4)
    for l in range(2):
        a = slice(128 * l, 128 * l + 128)
        V.tensor_tensor_scan(T.iotn[:, a], T.ones[:, 0:128], T.step[:, a], [63.0, 111.0][l], OP.mult, OP.add).then_inc(sem.ion, 1)
    V.wait_ge(sem.iod, 1)
    V.tensor_scalar(T.ident[:], T.diff[:], 0.0, None, OP.is_equal).then_inc(sem.vid, 1)
    r0 = slice(32 * rank, 32 * rank + 32)
    V.wait_ge(sem.dwr, 16)
    V.tensor_scalar(T.wf[:, 4:8], T.wi[:], -1.0, None, OP.mult).then_inc(sem.vwn, 1)
    V.tensor_copy(T.wf[:, 0:4], T.wi[:]).then_inc(sem.vwf, 1)
    cast_x(V, 0, 1)
    V.wait_ge(sem.dgv, 16)
    V.tensor_copy(T.giv[r0, :], T.gs[r0, :]).then_inc(sem.vgio, 1)
    turn_x(0, 1)
    V.wait_ge(sem.iol, 1)
    V.wait_ge(sem.vwf, 1)
    for i in range(2):
        V.tensor_scalar(T.vt[:, 256 * i:256 * i + 256], T.iotl[:], T.wf[:, i:i + 1], [64.0, 1.0][i],
                        OP.is_equal, OP.mult).then_inc(sem.vvt0, 1)
    V.wait_ge(sem.ion, 2)
    V.wait_ge(sem.vgio, 1)
    for k in range(2):
        V.tensor_scalar(T.gto[r0, 128 * k:128 * k + 128], T.iotn[r0, 0:128], T.giv[r0, k:k + 1], None,
                        OP.is_equal).then_inc(sem.vgto, 1)
    run(V, VE)
    V.wait_ge(sem.agv, ng * n_oth)
    for q in qs[1:]:
        V.tensor_copy(T.giv[32 * q:32 * q + 32, 0:4], T.gl[r0, 4 * q:4 * q + 4]).then_inc(sem.vgiv, 1)
    V.wait_ge(sem.vgiv, 3)
    onehot_give(0)
    run(V, VO)

    S.wait_ge(sem.iol, 1)
    S.wait_ge(sem.vwn, 1)
    for i in range(2):
        S.activation(T.vt[:, 512 + 256 * i:768 + 256 * i], T.iotl[:], ACT.Abs, bias=T.wf[:, 6 + i:7 + i]).then_inc(sem.sab, 1)
    for i in range(2):
        S.wait_ge(sem.sab, i + 1)
        a, top = T.vt[:, 512 + 256 * i:768 + 256 * i], [64.0, 1.0][i]
        S.activation(a, a, ACT.Relu, bias=top, scale=-top).then_inc(sem.vvt1, 1)
    S.wait_ge(sem.pv0, 2)
    copy(S, T.vb[:, 0:256], psv[0][:, 0:256]).then_inc(sem.sv0, 1)
    w_out(S, rank)
    S.wait_ge(sem.pv1, 2)
    copy(S, T.vb[:, 256:512], psv[1][:, 0:256]).then_inc(sem.sv1, 1)
    w_out(S, qs[2])
    run(S, SO)

    P.wait_ge(sem.vid, 1)
    compose_v(0)
    P.wait_ge(sem.sv0, 1)
    compose_w0([rank])
    compose_v(1)
    compose_w0(qs[1:])
    run(P, PO)

    for c in range(last + len(OUT)):
        store(Y, c)
    Y.wait_ge(sem.dy, 16 * nst[0])
